import numpy as np
CORES = [0,1,2,3,4,5,6,7]
N = 8
ROOT = 2
def setup_inputs(rng):
    return {"x": rng.standard_normal((N, 128, 4096), dtype=np.float32)}
def reference(x):
    y = np.full(x.shape, np.nan, x.dtype)
    y[ROOT] = x.min(axis=0)
    return {"y": y}

@@ -1,0 +1,82 @@
+from concourse.bass import DstId, RemoteDMATransfer
+
+COLS = 4096
+NSH = 7
+WMAX = -(-COLS // NSH)
+ALL16 = 16
+
+SCRATCH = {
+    "xs": ("sbuf", [128, COLS], "float32"),
+    "land": ("sbuf", [128, NSH * WMAX], "float32"),
+}
+SEMAPHORES = (["ld%d" % k for k in range(NSH)]
+              + ["res%d" % k for k in range(NSH)]
+              + ["arrived",
+                 "sent",
+                 "stored"])
+
+
+def shard_bounds():
+    base, extra = divmod(COLS, NSH)
+    out, a = [], 0
+    for k in range(NSH):
+        w = base + (1 if k < extra else 0)
+        out.append((a, a + w))
+        a += w
+    return out
+
+
+def rank_program(g, core, T, topo):
+    if T.rank_of(core) is None:
+        return
+    root = T.cores[T.root] if T.root is not None else 2
+    owners = [c for c in T.cores if c != root]
+    bounds = shard_bounds()
+    mine = owners.index(core) if core != root else None
+
+    start = (T.cores.index(core) + 1) % NSH
+    order = [(start + i) % NSH for i in range(NSH)]
+    order = [k for k in order if k != mine] + ([mine] if mine is not None else [])
+
+    local_q = [g.sync, g.scalar]
+    for i, k in enumerate(order):
+        a, b = bounds[k]
+        local_q[i % 2].dma_start(T.xs[:, a:b], T.x[:, a:b]).then_inc(T.sem["ld%d" % k], 16)
+
+    n_calls = 0
+    for k in order:
+        if k == mine:
+            continue
+        dst = owners[k]
+        a, b = bounds[k]
+        w = b - a
+        slot = [c for c in T.cores if c != dst].index(core)
+        rid, pid, _se = topo.addr(dst)
+        g.wait_ge(T.sem["ld%d" % k], 16)
+        g.remote_dma(T.land[:, slot * w:(slot + 1) * w], T.xs[:, a:b], T.sem.arrived, T.sem.sent,
+                     pid, rid, topo.mask(core, dst))
+        n_calls += 1
+
+    if mine is not None:
+        a, b = bounds[mine]
+        w = b - a
+        g.wait_ge(T.sem["ld%d" % mine], 16)
+        g.wait_ge(T.sem.arrived, NSH * ALL16)
+        rid, pid, _se = topo.addr(root)
+        g.remote_dma_fused([RemoteDMATransfer(
+            dst_ids=[DstId(rid=rid, pnc=pid)],
+            dma_engine_mask=topo.mask(core, root),
+            remote_sem=T.sem["res%d" % mine],
+            srcs=[T.land[:, i * w:(i + 1) * w] for i in range(NSH)] + [T.xs[:, a:b]],
+            dsts=[T.land[:, a:b]],
+            alu_op=3)], local_sem=T.sem.sent)
+        n_calls += 1
+    else:
+        for k in range(NSH):
+            a, b = bounds[k]
+            q = local_q[k % 2]
+            q.wait_ge(T.sem["res%d" % k], ALL16)
+            q.dma_start(T.y[:, a:b], T.land[:, a:b]).then_inc(T.sem.stored, 16)
+        g.wait_ge(T.sem.stored, NSH * 16)
+
+    g.wait_ge(T.sem.sent, n_calls * ALL16)

@@ -26,6 +26,12 @@ def shard_bounds():
     return out
 
 
+def send_order(mine):
+    if mine is None:
+        return list(range(NSH))
+    return [(2 * r - mine) % NSH for r in range(NSH) if r != mine]
+
+
 def rank_program(g, core, T, topo):
     if T.rank_of(core) is None:
         return
@@ -33,20 +39,15 @@ def rank_program(g, core, T, topo):
     owners = [c for c in T.cores if c != root]
     bounds = shard_bounds()
     mine = owners.index(core) if core != root else None
-
-    start = (T.cores.index(core) + 1) % NSH
-    order = [(start + i) % NSH for i in range(NSH)]
-    order = [k for k in order if k != mine] + ([mine] if mine is not None else [])
+    sends = send_order(mine)
 
     local_q = [g.sync, g.scalar]
-    for i, k in enumerate(order):
+    for i, k in enumerate(sends + ([mine] if mine is not None else [])):
         a, b = bounds[k]
         local_q[i % 2].dma_start(T.xs[:, a:b], T.x[:, a:b]).then_inc(T.sem["ld%d" % k], 16)
 
     n_calls = 0
-    for k in order:
-        if k == mine:
-            continue
+    for k in sends:
         dst = owners[k]
         a, b = bounds[k]
         w = b - a

from concourse.bass import DstId, RemoteDMATransfer

COLS = 4096
NSH = 7
WMAX = -(-COLS // NSH)
ALL16 = 16

SCRATCH = {
    "xs": ("sbuf", [128, COLS], "float32"),
    "land": ("sbuf", [128, NSH * WMAX], "float32"),
}
SEMAPHORES = (["ld%d" % k for k in range(NSH)]
              + ["res%d" % k for k in range(NSH)]
              + ["arrived",
                 "sent",
                 "stored"])


def shard_bounds():
    base, extra = divmod(COLS, NSH)
    out, a = [], 0
    for k in range(NSH):
        w = base + (1 if k < extra else 0)
        out.append((a, a + w))
        a += w
    return out


def send_order(mine):
    if mine is None:
        return list(range(NSH))
    return [(2 * r - mine) % NSH for r in range(NSH) if r != mine]


def rank_program(g, core, T, topo):
    if T.rank_of(core) is None:
        return
    root = T.cores[T.root] if T.root is not None else 2
    owners = [c for c in T.cores if c != root]
    bounds = shard_bounds()
    mine = owners.index(core) if core != root else None
    sends = send_order(mine)

    local_q = [g.sync, g.scalar]
    for i, k in enumerate(sends + ([mine] if mine is not None else [])):
        a, b = bounds[k]
        local_q[i % 2].dma_start(T.xs[:, a:b], T.x[:, a:b]).then_inc(T.sem["ld%d" % k], 16)

    n_calls = 0
    for k in sends:
        dst = owners[k]
        a, b = bounds[k]
        w = b - a
        slot = [c for c in T.cores if c != dst].index(core)
        rid, pid, _se = topo.addr(dst)
        g.wait_ge(T.sem["ld%d" % k], 16)
        g.remote_dma(T.land[:, slot * w:(slot + 1) * w], T.xs[:, a:b], T.sem.arrived, T.sem.sent,
                     pid, rid, topo.mask(core, dst))
        n_calls += 1

    if mine is not None:
        a, b = bounds[mine]
        w = b - a
        g.wait_ge(T.sem["ld%d" % mine], 16)
        g.wait_ge(T.sem.arrived, NSH * ALL16)
        rid, pid, _se = topo.addr(root)
        g.remote_dma_fused([RemoteDMATransfer(
            dst_ids=[DstId(rid=rid, pnc=pid)],
            dma_engine_mask=topo.mask(core, root),
            remote_sem=T.sem["res%d" % mine],
            srcs=[T.land[:, i * w:(i + 1) * w] for i in range(NSH)] + [T.xs[:, a:b]],
            dsts=[T.land[:, a:b]],
            alu_op=3)], local_sem=T.sem.sent)
        n_calls += 1
    else:
        for k in range(NSH):
            a, b = bounds[k]
            q = local_q[k % 2]
            q.wait_ge(T.sem["res%d" % k], ALL16)
            q.dma_start(T.y[:, a:b], T.land[:, a:b]).then_inc(T.sem.stored, 16)
        g.wait_ge(T.sem.stored, NSH * 16)

    g.wait_ge(T.sem.sent, n_calls * ALL16)
